import numpy as np, ml_dtypes
CORES = [78,86,94,102,110,118]
N = 6
TK = 512
def setup_inputs(rng):
    rt = (0.75 * rng.standard_normal((128, 1), dtype=np.float32) + rng.standard_normal((128, N), dtype=np.float32) / 2).astype(ml_dtypes.bfloat16)
    return {"x": rng.standard_normal((N, 128, TK), dtype=np.float32).astype(ml_dtypes.bfloat16), "rt": np.broadcast_to(rt, (N, 128, N)).copy(), "w": rng.standard_normal((N, 128, 128), dtype=np.float32).astype(ml_dtypes.bfloat16)}
def setup_inputs_big(rng):
    d = setup_inputs(rng)
    for k in ("x", "w"): d[k] = (d[k].astype(np.float32) * 1024.0).astype(d[k].dtype)
    return d
def setup_inputs_small(rng):
    d = setup_inputs(rng)
    for k in ("x", "w"): d[k] = (d[k].astype(np.float32) * (1 / 1024.0)).astype(d[k].dtype)
    return d
def reference(x, rt, w):
    X, RT, W = x.astype(np.float64), rt.astype(np.float64), w.astype(np.float64)
    y = np.zeros((N, 128, TK))
    for r in range(N):
        sc = RT[r].T @ X[r]
        g = np.exp(sc - sc.max(axis=0)); g = g / g.sum(axis=0)
        y[r] = sum(g[j] * (W[j].T @ X[r]) for j in range(N))
    return {"y": y.astype(ml_dtypes.bfloat16)}

@@ -1,0 +1,153 @@
+from concourse.bass import DstId, RemoteDMATransfer
+from concourse.mybir import AluOpType, AxisListType, ActivationFunctionType
+
+N = 6
+TK = 512
+NB = 4
+BF = "bfloat16"
+F32 = "float32"
+
+SCRATCH = {
+    "xs": ("sbuf", [128, TK], BF),
+    "rts": ("sbuf", [128, N], BF),
+    "wall": ("sbuf", [128, N * 128], BF),
+    "ones": ("sbuf", [128, 128], BF),
+    "ident": ("sbuf", [128, 128], BF),
+    "negm": ("sbuf", [128, NB], F32),
+    "esum": ("sbuf", [128, NB], F32),
+    "rs": ("sbuf", [128, NB], F32),
+    "et": ("sbuf", [128, NB * N], F32),
+    "dr": ("sbuf", [128, TK], BF),
+    "zg": ("sbuf", [128, TK], BF),
+    "lrep": ("sbuf", [128, (N - 1) * TK], BF),
+    "gx": ("sbuf", [128, (N - 1) * TK], BF),
+    "ys": ("sbuf", [128, TK], BF),
+    "pa": ("psum", [128, 512], F32),
+    "pb": ("psum", [128, 512], F32),
+    "pc": ("psum", [128, 512], F32),
+    "pd": ("psum", [128, 512], F32),
+    "y0": ("psum", [128, 512], F32),
+    "y1": ("psum", [128, 512], F32),
+    "y2": ("psum", [128, 512], F32),
+    "y3": ("psum", [128, 512], F32),
+}
+SEMAPHORES = ["s_w", "s_rt", "s_x", "s_ones", "s_id", "s_st", "s_mx", "s_ex", "s_rc", "s_dr", "s_z", "s_zg", "s_l",
+              "s_gb", "s_gx", "s_y", "s_ev0", "s_ev1", "s_o0", "s_o1", "s_sent"] + ["arr%d" % j for j in range(N)]
+
+
+def rank_program(g, core, T, topo):
+    rank = T.rank_of(core)
+    if rank is None:
+        return
+    S = T.sem
+    pe, dve, act, sp = g.tensor, g.vector, g.scalar, g.sync
+    Copy, Exp = ActivationFunctionType.Copy, ActivationFunctionType.Exp
+
+    def blk(t, i, w=128):
+        return t[:, i * w:(i + 1) * w]
+
+    dests = [(rank + k) % N for k in range(1, N)]
+    order = [(rank - k) % N for k in range(1, N)]
+    mask = topo.mask(core, T.cores[dests[0]])
+    for d in dests:
+        if not topo.may_write(core, T.cores[d]):
+            raise ValueError("rank core cannot reach a destination directly")
+        mask &= topo.mask(core, T.cores[d])
+    ne = bin(mask).count("1")
+
+    sp.dma_start(blk(T.wall, rank), T.w[:, :]).then_inc(S.s_w, 16)
+    act.dma_start(T.xs[:, :], T.x[:, :]).then_inc(S.s_x, 16)
+    sp.dma_start(T.rts[:, :], T.rt[:, :]).then_inc(S.s_rt, 16)
+
+    dve.memset(T.ones[:, :], 1.0).then_inc(S.s_ones, 1)
+    g.wait_ge(S.s_ones, 1)
+    g.affine_select(T.ident[:, :], T.ones[:, :], [[-1, 128]], AluOpType.is_equal, 0.0, 0, 1).then_inc(S.s_id, 1)
+
+    g.wait_ge(S.s_w, 16)
+    ids = []
+    for d in dests:
+        rid, pid, _se = topo.addr(T.cores[d])
+        ids.append(DstId(rid=rid, pnc=pid))
+    g.remote_dma_fused([RemoteDMATransfer(dst_ids=ids, dma_engine_mask=mask, remote_sem=S["arr%d" % rank],
+                                          srcs=[blk(T.wall, rank)], dsts=[blk(T.wall, rank) for _ in dests],
+                                          alu_op=0)], local_sem=S.s_sent)
+
+    pe.wait_ge(S.s_x, 16)
+    pe.wait_ge(S.s_rt, 16)
+    for c in range(NB):
+        pe.matmul(blk(T.pa, c, N), blk(T.xs, c), T.rts[:, :], True, True).then_inc(S.s_st, 1)
+    pe.wait_ge(S.s_w, 16)
+    for c in range(NB):
+        pe.matmul(blk(T.pb, c), blk(T.xs, c), blk(T.wall, rank), True, True).then_inc(S.s_z, 1)
+
+    dve.wait_ge(S.s_st, NB)
+    for c in range(NB):
+        dve.tensor_reduce(T.negm[:, c:c + 1], blk(T.pa, c, N), AxisListType.X, AluOpType.max,
+                          negate=True).then_inc(S.s_mx, 1)
+    act.wait_ge(S.s_mx, NB)
+    for c in range(NB):
+        act.activation(blk(T.et, c, N), blk(T.pa, c, N), Exp, bias=T.negm[:, c:c + 1], scale=1.0,
+                       accum_out=T.esum[:, c:c + 1]).then_inc(S.s_ex, 1)
+    dve.wait_ge(S.s_ex, NB)
+    dve.reciprocal(T.rs[:, :], T.esum[:, :]).then_inc(S.s_rc, 1)
+    dve.wait_ge(S.s_rc, 1)
+    dve.wait_ge(S.s_id, 1)
+    for c in range(NB):
+        dve.tensor_scalar(blk(T.dr, c), T.ident[:, :], T.rs[:, c:c + 1], None, AluOpType.mult).then_inc(S.s_dr, 1)
+
+    act.wait_ge(S.s_ex, NB)
+    act.wait_ge(S.s_z, NB)
+    for c in range(NB):
+        col = c * N + rank
+        act.activation(blk(T.zg, c), blk(T.pb, c), Copy, scale=T.et[:, col:col + 1]).then_inc(S.s_zg, 1)
+    act.wait_ge(S.s_ones, 1)
+    for k, j in enumerate(order):
+        for c in range(NB):
+            col = c * N + j
+            act.activation(blk(T.lrep, k * NB + c), T.ones[:, :], Copy,
+                           scale=T.et[:, col:col + 1]).then_inc(S.s_l, 1)
+
+    ybank = [T.y0, T.y1, T.y2, T.y3]
+    for c in range(NB):
+        pe.wait_ge(S.s_dr, c + 1)
+        pe.wait_ge(S.s_zg, c + 1)
+        pe.matmul(ybank[c][:, 0:128], blk(T.zg, c), blk(T.dr, c), True, False)
+    gbank = [T.pc, T.pd, T.pa, T.pb]
+    for k in range(N - 1):
+        if k >= len(gbank):
+            pe.wait_ge(S.s_gx, k - len(gbank) + 1)
+        for c in range(NB):
+            pe.wait_ge(S.s_l, k * NB + c + 1)
+            pe.matmul(blk(gbank[k % len(gbank)], c), blk(T.lrep, k * NB + c), blk(T.dr, c), True,
+                      True).then_inc(S.s_gb, 1)
+
+    dve.wait_ge(S.s_x, 16)
+    for k in range(N - 1):
+        dve.wait_ge(S.s_gb, (k + 1) * NB)
+        dve.tensor_tensor(blk(T.gx, k, TK), T.xs[:, :], gbank[k % len(gbank)][:, :],
+                          AluOpType.mult).then_inc(S.s_gx, 1)
+
+    for k, j in enumerate(order):
+        pe.wait_ge(S.s_gx, k + 1)
+        pe.wait_ge(S["arr%d" % j], ne)
+        last = k == N - 2
+        for c in range(NB):
+            mm = pe.matmul(ybank[c][:, 0:128], blk(T.wall, j), blk(T.gx, k * NB + c), False, last)
+            if last:
+                mm.then_inc(S.s_y, 1)
+
+    ev = [S.s_ev0, S.s_ev0, S.s_ev1, S.s_ev1]
+    for c in range(NB):
+        if c % 2 == 0:
+            dve.wait_ge(S.s_y, c + 1)
+            dve.tensor_copy(blk(T.ys, c), ybank[c][:, 0:128]).then_inc(ev[c], 1)
+        else:
+            act.wait_ge(S.s_y, c + 1)
+            act.activation(blk(T.ys, c), ybank[c][:, 0:128], Copy).then_inc(ev[c], 1)
+    sp.wait_ge(S.s_ev0, 2)
+    sp.dma_start(T.y[:, 0:256], T.ys[:, 0:256]).then_inc(S.s_o0, 16)
+    act.wait_ge(S.s_ev1, 2)
+    act.dma_start(T.y[:, 256:512], T.ys[:, 256:512]).then_inc(S.s_o1, 16)
+    sp.wait_ge(S.s_o0, 16)
+    act.wait_ge(S.s_o1, 16)
+    g.wait_ge(S.s_sent, ne)

@@ -18,21 +18,19 @@ SCRATCH = {
     "rs": ("sbuf", [128, NB], F32),
     "et": ("sbuf", [128, NB * N], F32),
     "dr": ("sbuf", [128, TK], BF),
-    "zg": ("sbuf", [128, TK], BF),
-    "lrep": ("sbuf", [128, (N - 1) * TK], BF),
-    "gx": ("sbuf", [128, (N - 1) * TK], BF),
+    "zg": ("sbuf", [128, N * TK], BF),
     "ys": ("sbuf", [128, TK], BF),
     "pa": ("psum", [128, 512], F32),
-    "pb": ("psum", [128, 512], F32),
-    "pc": ("psum", [128, 512], F32),
-    "pd": ("psum", [128, 512], F32),
+    "pz0": ("psum", [128, 512], F32),
+    "pz1": ("psum", [128, 512], F32),
+    "pz2": ("psum", [128, 512], F32),
     "y0": ("psum", [128, 512], F32),
     "y1": ("psum", [128, 512], F32),
     "y2": ("psum", [128, 512], F32),
     "y3": ("psum", [128, 512], F32),
 }
-SEMAPHORES = ["s_w", "s_rt", "s_x", "s_ones", "s_id", "s_st", "s_mx", "s_ex", "s_rc", "s_dr", "s_z", "s_zg", "s_l",
-              "s_gb", "s_gx", "s_y", "s_ev0", "s_ev1", "s_o0", "s_o1", "s_sent"] + ["arr%d" % j for j in range(N)]
+SEMAPHORES = ["s_w", "s_rt", "s_x", "s_ones", "s_id", "s_st", "s_mx", "s_ex", "s_rc", "s_dr", "s_zz", "s_ga", "s_gd",
+              "s_y", "s_ev0", "s_ev1", "s_o0", "s_o1", "s_sent"] + ["arr%d" % j for j in range(N)]
 
 
 def rank_program(g, core, T, topo):
@@ -47,13 +45,23 @@ def rank_program(g, core, T, topo):
         return t[:, i * w:(i + 1) * w]
 
     dests = [(rank + k) % N for k in range(1, N)]
-    order = [(rank - k) % N for k in range(1, N)]
+    experts = [rank] + [(rank - k) % N for k in range(1, N)]
     mask = topo.mask(core, T.cores[dests[0]])
     for d in dests:
         if not topo.may_write(core, T.cores[d]):
             raise ValueError("rank core cannot reach a destination directly")
         mask &= topo.mask(core, T.cores[d])
     ne = bin(mask).count("1")
+
+    ybank = [T.y0, T.y1, T.y2, T.y3]
+    zbank = [T.pz0, T.pz1, T.pz2, T.pa]
+
+    def gated(k, c):
+        if k == 0:
+            return S.s_ga, c + 1
+        if c < 2:
+            return S.s_ga, NB + 2 * (k - 1) + c + 1
+        return S.s_gd, 2 * (k - 1) + (c - 2) + 1
 
     sp.dma_start(blk(T.wall, rank), T.w[:, :]).then_inc(S.s_w, 16)
     act.dma_start(T.xs[:, :], T.x[:, :]).then_inc(S.s_x, 16)
@@ -76,10 +84,6 @@ def rank_program(g, core, T, topo):
     pe.wait_ge(S.s_rt, 16)
     for c in range(NB):
         pe.matmul(blk(T.pa, c, N), blk(T.xs, c), T.rts[:, :], True, True).then_inc(S.s_st, 1)
-    pe.wait_ge(S.s_w, 16)
-    for c in range(NB):
-        pe.matmul(blk(T.pb, c), blk(T.xs, c), blk(T.wall, rank), True, True).then_inc(S.s_z, 1)
-
     dve.wait_ge(S.s_st, NB)
     for c in range(NB):
         dve.tensor_reduce(T.negm[:, c:c + 1], blk(T.pa, c, N), AxisListType.X, AluOpType.max,
@@ -88,6 +92,7 @@ def rank_program(g, core, T, topo):
     for c in range(NB):
         act.activation(blk(T.et, c, N), blk(T.pa, c, N), Exp, bias=T.negm[:, c:c + 1], scale=1.0,
                        accum_out=T.esum[:, c:c + 1]).then_inc(S.s_ex, 1)
+    act.wait_ge(S.s_ex, NB)
     dve.wait_ge(S.s_ex, NB)
     dve.reciprocal(T.rs[:, :], T.esum[:, :]).then_inc(S.s_rc, 1)
     dve.wait_ge(S.s_rc, 1)
@@ -95,46 +100,43 @@ def rank_program(g, core, T, topo):
     for c in range(NB):
         dve.tensor_scalar(blk(T.dr, c), T.ident[:, :], T.rs[:, c:c + 1], None, AluOpType.mult).then_inc(S.s_dr, 1)
 
-    act.wait_ge(S.s_ex, NB)
-    act.wait_ge(S.s_z, NB)
-    for c in range(NB):
-        col = c * N + rank
-        act.activation(blk(T.zg, c), blk(T.pb, c), Copy, scale=T.et[:, col:col + 1]).then_inc(S.s_zg, 1)
-    act.wait_ge(S.s_ones, 1)
-    for k, j in enumerate(order):
+    def turn(k):
         for c in range(NB):
-            col = c * N + j
-            act.activation(blk(T.lrep, k * NB + c), T.ones[:, :], Copy,
-                           scale=T.et[:, col:col + 1]).then_inc(S.s_l, 1)
-
-    ybank = [T.y0, T.y1, T.y2, T.y3]
-    for c in range(NB):
-        pe.wait_ge(S.s_dr, c + 1)
-        pe.wait_ge(S.s_zg, c + 1)
-        pe.matmul(ybank[c][:, 0:128], blk(T.zg, c), blk(T.dr, c), True, False)
-    gbank = [T.pc, T.pd, T.pa, T.pb]
-    for k in range(N - 1):
-        if k >= len(gbank):
-            pe.wait_ge(S.s_gx, k - len(gbank) + 1)
-        for c in range(NB):
-            pe.wait_ge(S.s_l, k * NB + c + 1)
-            pe.matmul(blk(gbank[k % len(gbank)], c), blk(T.lrep, k * NB + c), blk(T.dr, c), True,
-                      True).then_inc(S.s_gb, 1)
-
-    dve.wait_ge(S.s_x, 16)
-    for k in range(N - 1):
-        dve.wait_ge(S.s_gb, (k + 1) * NB)
-        dve.tensor_tensor(blk(T.gx, k, TK), T.xs[:, :], gbank[k % len(gbank)][:, :],
-                          AluOpType.mult).then_inc(S.s_gx, 1)
-
-    for k, j in enumerate(order):
-        pe.wait_ge(S.s_gx, k + 1)
-        pe.wait_ge(S["arr%d" % j], ne)
-        last = k == N - 2
-        for c in range(NB):
-            mm = pe.matmul(ybank[c][:, 0:128], blk(T.wall, j), blk(T.gx, k * NB + c), False, last)
-            if last:
+            sem, cnt = gated(k, c)
+            pe.wait_ge(sem, cnt)
+            mm = pe.matmul(ybank[c][:, 0:128], blk(T.zg, k * NB + c), blk(T.dr, c), k == 0, k == N - 1)
+            if k == N - 1:
                 mm.then_inc(S.s_y, 1)
+
+    for k, j in enumerate(experts):
+        pe.wait_ge(S.s_w, 16) if k == 0 else pe.wait_ge(S["arr%d" % j], ne)
+        for h in range(2):
+            zb = zbank[(2 * k + h) % 4]
+            if k >= 2:
+                sem, cnt = gated(k - 2, 2 * h + 1)
+                pe.wait_ge(sem, cnt)
+            elif k == 1 and h == 1:
+                pe.wait_ge(S.s_ex, NB)
+            for b in range(2):
+                pe.matmul(blk(zb, b), blk(T.xs, 2 * h + b), blk(T.wall, j), True, True).then_inc(S.s_zz, 1)
+        for h in range(2):
+            zb = zbank[(2 * k + h) % 4]
+            on_act = k == 0 or h == 0
+            (act if on_act else dve).wait_ge(S.s_zz, NB * k + 2 * h + 2)
+            for b in range(2):
+                c = 2 * h + b
+                col = c * N + j
+                if on_act:
+                    act.activation(blk(T.zg, k * NB + c), blk(zb, b), Copy,
+                                   scale=T.et[:, col:col + 1]).then_inc(S.s_ga, 1)
+                else:
+                    dve.tensor_scalar(blk(T.zg, k * NB + c), blk(zb, b), T.et[:, col:col + 1], None,
+                                      AluOpType.mult).then_inc(S.s_gd, 1)
+        if k == 1:
+            pe.wait_ge(S.s_dr, NB)
+        if k >= 1:
+            turn(k - 1)
+    turn(N - 1)
 
     ev = [S.s_ev0, S.s_ev0, S.s_ev1, S.s_ev1]
     for c in range(NB):

@@ -4,6 +4,7 @@ from concourse.mybir import AluOpType, AxisListType, ActivationFunctionType
 N = 6
 TK = 512
 NB = 4
+LAG = 2
 BF = "bfloat16"
 F32 = "float32"
 
@@ -20,17 +21,17 @@ SCRATCH = {
     "dr": ("sbuf", [128, TK], BF),
     "zg": ("sbuf", [128, N * TK], BF),
     "ys": ("sbuf", [128, TK], BF),
-    "pa": ("psum", [128, 512], F32),
     "pz0": ("psum", [128, 512], F32),
     "pz1": ("psum", [128, 512], F32),
     "pz2": ("psum", [128, 512], F32),
+    "pz3": ("psum", [128, 512], F32),
     "y0": ("psum", [128, 512], F32),
     "y1": ("psum", [128, 512], F32),
     "y2": ("psum", [128, 512], F32),
     "y3": ("psum", [128, 512], F32),
 }
-SEMAPHORES = ["s_w", "s_rt", "s_x", "s_ones", "s_id", "s_st", "s_mx", "s_ex", "s_rc", "s_dr", "s_zz", "s_ga", "s_gd",
-              "s_y", "s_ev0", "s_ev1", "s_o0", "s_o1", "s_sent"] + ["arr%d" % j for j in range(N)]
+SEMAPHORES = ["s_w", "s_rt", "s_x0", "s_x", "s_ones", "s_id", "s_st0", "s_st", "s_mx0", "s_mx", "s_ex", "s_rc", "s_dr",
+              "s_zz", "s_ga", "s_gd", "s_y", "s_ev0", "s_ev1", "s_o0", "s_o1", "s_sent"] + ["arr%d" % j for j in range(N)]
 
 
 def rank_program(g, core, T, topo):
@@ -54,7 +55,7 @@ def rank_program(g, core, T, topo):
     ne = bin(mask).count("1")
 
     ybank = [T.y0, T.y1, T.y2, T.y3]
-    zbank = [T.pz0, T.pz1, T.pz2, T.pa]
+    zbank = [T.pz0, T.pz1, T.pz2, T.pz3]
 
     def gated(k, c):
         if k == 0:
@@ -63,9 +64,13 @@ def rank_program(g, core, T, topo):
             return S.s_ga, NB + 2 * (k - 1) + c + 1
         return S.s_gd, 2 * (k - 1) + (c - 2) + 1
 
+    def scores(c):
+        return T.y3[:, 0:N] if c == 0 else blk(T.y2, c, N)
+
     sp.dma_start(blk(T.wall, rank), T.w[:, :]).then_inc(S.s_w, 16)
-    act.dma_start(T.xs[:, :], T.x[:, :]).then_inc(S.s_x, 16)
+    act.dma_start(T.xs[:, 0:128], T.x[:, 0:128]).then_inc(S.s_x0, 16)
     sp.dma_start(T.rts[:, :], T.rt[:, :]).then_inc(S.s_rt, 16)
+    act.dma_start(T.xs[:, 128:TK], T.x[:, 128:TK]).then_inc(S.s_x, 16)
 
     dve.memset(T.ones[:, :], 1.0).then_inc(S.s_ones, 1)
     g.wait_ge(S.s_ones, 1)
@@ -80,17 +85,25 @@ def rank_program(g, core, T, topo):
                                           srcs=[blk(T.wall, rank)], dsts=[blk(T.wall, rank) for _ in dests],
                                           alu_op=0)], local_sem=S.s_sent)
 
-    pe.wait_ge(S.s_x, 16)
+    pe.wait_ge(S.s_x0, 16)
     pe.wait_ge(S.s_rt, 16)
+    pe.matmul(scores(0), blk(T.xs, 0), T.rts[:, :], True, True).then_inc(S.s_st0, 1)
+    pe.wait_ge(S.s_x, 16)
+    for c in range(1, NB):
+        pe.matmul(scores(c), blk(T.xs, c), T.rts[:, :], True, True).then_inc(S.s_st, 1)
     for c in range(NB):
-        pe.matmul(blk(T.pa, c, N), blk(T.xs, c), T.rts[:, :], True, True).then_inc(S.s_st, 1)
-    dve.wait_ge(S.s_st, NB)
+        if c == 0:
+            dve.wait_ge(S.s_st0, 1)
+        elif c == 1:
+            dve.wait_ge(S.s_st, NB - 1)
+        dve.tensor_reduce(T.negm[:, c:c + 1], scores(c), AxisListType.X, AluOpType.max,
+                          negate=True).then_inc(S.s_mx0 if c == 0 else S.s_mx, 1)
     for c in range(NB):
-        dve.tensor_reduce(T.negm[:, c:c + 1], blk(T.pa, c, N), AxisListType.X, AluOpType.max,
-                          negate=True).then_inc(S.s_mx, 1)
-    act.wait_ge(S.s_mx, NB)
-    for c in range(NB):
-        act.activation(blk(T.et, c, N), blk(T.pa, c, N), Exp, bias=T.negm[:, c:c + 1], scale=1.0,
+        if c == 0:
+            act.wait_ge(S.s_mx0, 1)
+        elif c == 1:
+            act.wait_ge(S.s_mx, NB - 1)
+        act.activation(blk(T.et, c, N), scores(c), Exp, bias=T.negm[:, c:c + 1], scale=1.0,
                        accum_out=T.esum[:, c:c + 1]).then_inc(S.s_ex, 1)
     act.wait_ge(S.s_ex, NB)
     dve.wait_ge(S.s_ex, NB)
@@ -102,6 +115,8 @@ def rank_program(g, core, T, topo):
 
     def turn(k):
         for c in range(NB):
+            if k == 0:
+                pe.wait_ge(S.s_dr, c + 1)
             sem, cnt = gated(k, c)
             pe.wait_ge(sem, cnt)
             mm = pe.matmul(ybank[c][:, 0:128], blk(T.zg, k * NB + c), blk(T.dr, c), k == 0, k == N - 1)
@@ -115,8 +130,6 @@ def rank_program(g, core, T, topo):
             if k >= 2:
                 sem, cnt = gated(k - 2, 2 * h + 1)
                 pe.wait_ge(sem, cnt)
-            elif k == 1 and h == 1:
-                pe.wait_ge(S.s_ex, NB)
             for b in range(2):
                 pe.matmul(blk(zb, b), blk(T.xs, 2 * h + b), blk(T.wall, j), True, True).then_inc(S.s_zz, 1)
         for h in range(2):
@@ -132,11 +145,10 @@ def rank_program(g, core, T, topo):
                 else:
                     dve.tensor_scalar(blk(T.zg, k * NB + c), blk(zb, b), T.et[:, col:col + 1], None,
                                       AluOpType.mult).then_inc(S.s_gd, 1)
-        if k == 1:
-            pe.wait_ge(S.s_dr, NB)
-        if k >= 1:
-            turn(k - 1)
-    turn(N - 1)
+        if k >= LAG:
+            turn(k - LAG)
+    for k in range(N - LAG, N):
+        turn(k)
 
     ev = [S.s_ev0, S.s_ev0, S.s_ev1, S.s_ev1]
     for c in range(NB):

from concourse.bass import DstId, RemoteDMATransfer
from concourse.mybir import AluOpType, AxisListType, ActivationFunctionType

N = 6
TK = 512
NB = 4
LAG = 2
BF = "bfloat16"
F32 = "float32"

SCRATCH = {
    "xs": ("sbuf", [128, TK], BF),
    "rts": ("sbuf", [128, N], BF),
    "wall": ("sbuf", [128, N * 128], BF),
    "ones": ("sbuf", [128, 128], BF),
    "ident": ("sbuf", [128, 128], BF),
    "negm": ("sbuf", [128, NB], F32),
    "esum": ("sbuf", [128, NB], F32),
    "rs": ("sbuf", [128, NB], F32),
    "et": ("sbuf", [128, NB * N], F32),
    "dr": ("sbuf", [128, TK], BF),
    "zg": ("sbuf", [128, N * TK], BF),
    "ys": ("sbuf", [128, TK], BF),
    "pz0": ("psum", [128, 512], F32),
    "pz1": ("psum", [128, 512], F32),
    "pz2": ("psum", [128, 512], F32),
    "pz3": ("psum", [128, 512], F32),
    "y0": ("psum", [128, 512], F32),
    "y1": ("psum", [128, 512], F32),
    "y2": ("psum", [128, 512], F32),
    "y3": ("psum", [128, 512], F32),
}
SEMAPHORES = ["s_w", "s_rt", "s_x0", "s_x", "s_ones", "s_id", "s_st0", "s_st", "s_mx0", "s_mx", "s_ex", "s_rc", "s_dr",
              "s_zz", "s_ga", "s_gd", "s_y", "s_ev0", "s_ev1", "s_o0", "s_o1", "s_sent"] + ["arr%d" % j for j in range(N)]


def rank_program(g, core, T, topo):
    rank = T.rank_of(core)
    if rank is None:
        return
    S = T.sem
    pe, dve, act, sp = g.tensor, g.vector, g.scalar, g.sync
    Copy, Exp = ActivationFunctionType.Copy, ActivationFunctionType.Exp

    def blk(t, i, w=128):
        return t[:, i * w:(i + 1) * w]

    dests = [(rank + k) % N for k in range(1, N)]
    experts = [rank] + [(rank - k) % N for k in range(1, N)]
    mask = topo.mask(core, T.cores[dests[0]])
    for d in dests:
        if not topo.may_write(core, T.cores[d]):
            raise ValueError("rank core cannot reach a destination directly")
        mask &= topo.mask(core, T.cores[d])
    ne = bin(mask).count("1")

    ybank = [T.y0, T.y1, T.y2, T.y3]
    zbank = [T.pz0, T.pz1, T.pz2, T.pz3]

    def gated(k, c):
        if k == 0:
            return S.s_ga, c + 1
        if c < 2:
            return S.s_ga, NB + 2 * (k - 1) + c + 1
        return S.s_gd, 2 * (k - 1) + (c - 2) + 1

    def scores(c):
        return T.y3[:, 0:N] if c == 0 else blk(T.y2, c, N)

    sp.dma_start(blk(T.wall, rank), T.w[:, :]).then_inc(S.s_w, 16)
    act.dma_start(T.xs[:, 0:128], T.x[:, 0:128]).then_inc(S.s_x0, 16)
    sp.dma_start(T.rts[:, :], T.rt[:, :]).then_inc(S.s_rt, 16)
    act.dma_start(T.xs[:, 128:TK], T.x[:, 128:TK]).then_inc(S.s_x, 16)

    dve.memset(T.ones[:, :], 1.0).then_inc(S.s_ones, 1)
    g.wait_ge(S.s_ones, 1)
    g.affine_select(T.ident[:, :], T.ones[:, :], [[-1, 128]], AluOpType.is_equal, 0.0, 0, 1).then_inc(S.s_id, 1)

    g.wait_ge(S.s_w, 16)
    ids = []
    for d in dests:
        rid, pid, _se = topo.addr(T.cores[d])
        ids.append(DstId(rid=rid, pnc=pid))
    g.remote_dma_fused([RemoteDMATransfer(dst_ids=ids, dma_engine_mask=mask, remote_sem=S["arr%d" % rank],
                                          srcs=[blk(T.wall, rank)], dsts=[blk(T.wall, rank) for _ in dests],
                                          alu_op=0)], local_sem=S.s_sent)

    pe.wait_ge(S.s_x0, 16)
    pe.wait_ge(S.s_rt, 16)
    pe.matmul(scores(0), blk(T.xs, 0), T.rts[:, :], True, True).then_inc(S.s_st0, 1)
    pe.wait_ge(S.s_x, 16)
    for c in range(1, NB):
        pe.matmul(scores(c), blk(T.xs, c), T.rts[:, :], True, True).then_inc(S.s_st, 1)
    for c in range(NB):
        if c == 0:
            dve.wait_ge(S.s_st0, 1)
        elif c == 1:
            dve.wait_ge(S.s_st, NB - 1)
        dve.tensor_reduce(T.negm[:, c:c + 1], scores(c), AxisListType.X, AluOpType.max,
                          negate=True).then_inc(S.s_mx0 if c == 0 else S.s_mx, 1)
    for c in range(NB):
        if c == 0:
            act.wait_ge(S.s_mx0, 1)
        elif c == 1:
            act.wait_ge(S.s_mx, NB - 1)
        act.activation(blk(T.et, c, N), scores(c), Exp, bias=T.negm[:, c:c + 1], scale=1.0,
                       accum_out=T.esum[:, c:c + 1]).then_inc(S.s_ex, 1)
    act.wait_ge(S.s_ex, NB)
    dve.wait_ge(S.s_ex, NB)
    dve.reciprocal(T.rs[:, :], T.esum[:, :]).then_inc(S.s_rc, 1)
    dve.wait_ge(S.s_rc, 1)
    dve.wait_ge(S.s_id, 1)
    for c in range(NB):
        dve.tensor_scalar(blk(T.dr, c), T.ident[:, :], T.rs[:, c:c + 1], None, AluOpType.mult).then_inc(S.s_dr, 1)

    def turn(k):
        for c in range(NB):
            if k == 0:
                pe.wait_ge(S.s_dr, c + 1)
            sem, cnt = gated(k, c)
            pe.wait_ge(sem, cnt)
            mm = pe.matmul(ybank[c][:, 0:128], blk(T.zg, k * NB + c), blk(T.dr, c), k == 0, k == N - 1)
            if k == N - 1:
                mm.then_inc(S.s_y, 1)

    for k, j in enumerate(experts):
        pe.wait_ge(S.s_w, 16) if k == 0 else pe.wait_ge(S["arr%d" % j], ne)
        for h in range(2):
            zb = zbank[(2 * k + h) % 4]
            if k >= 2:
                sem, cnt = gated(k - 2, 2 * h + 1)
                pe.wait_ge(sem, cnt)
            for b in range(2):
                pe.matmul(blk(zb, b), blk(T.xs, 2 * h + b), blk(T.wall, j), True, True).then_inc(S.s_zz, 1)
        for h in range(2):
            zb = zbank[(2 * k + h) % 4]
            on_act = k == 0 or h == 0
            (act if on_act else dve).wait_ge(S.s_zz, NB * k + 2 * h + 2)
            for b in range(2):
                c = 2 * h + b
                col = c * N + j
                if on_act:
                    act.activation(blk(T.zg, k * NB + c), blk(zb, b), Copy,
                                   scale=T.et[:, col:col + 1]).then_inc(S.s_ga, 1)
                else:
                    dve.tensor_scalar(blk(T.zg, k * NB + c), blk(zb, b), T.et[:, col:col + 1], None,
                                      AluOpType.mult).then_inc(S.s_gd, 1)
        if k >= LAG:
            turn(k - LAG)
    for k in range(N - LAG, N):
        turn(k)

    ev = [S.s_ev0, S.s_ev0, S.s_ev1, S.s_ev1]
    for c in range(NB):
        if c % 2 == 0:
            dve.wait_ge(S.s_y, c + 1)
            dve.tensor_copy(blk(T.ys, c), ybank[c][:, 0:128]).then_inc(ev[c], 1)
        else:
            act.wait_ge(S.s_y, c + 1)
            act.activation(blk(T.ys, c), ybank[c][:, 0:128], Copy).then_inc(ev[c], 1)
    sp.wait_ge(S.s_ev0, 2)
    sp.dma_start(T.y[:, 0:256], T.ys[:, 0:256]).then_inc(S.s_o0, 16)
    act.wait_ge(S.s_ev1, 2)
    act.dma_start(T.y[:, 256:512], T.ys[:, 256:512]).then_inc(S.s_o1, 16)
    sp.wait_ge(S.s_o0, 16)
    act.wait_ge(S.s_o1, 16)
    g.wait_ge(S.s_sent, ne)
